import numpy as np
import ml_dtypes


def mxq(x, axis, fmt="e4m3"):
    dtype, down = {"e4m3": (ml_dtypes.float8_e4m3fn, 7), "e5m2": (ml_dtypes.float8_e5m2, 14)}[fmt]
    v = np.moveaxis(np.asarray(x, np.float32).astype(ml_dtypes.bfloat16).astype(np.float64), axis, -1)
    blocks = v.reshape(v.shape[:-1] + (-1, 32))
    amax = np.abs(blocks).max(-1, keepdims=True)
    byte = np.maximum(np.where(amax > 0, np.frexp(amax)[1] - 1 + 127, 0) - down, 1)
    scale = np.exp2(byte - 127.0)
    codes = (blocks / scale).astype(np.float32).astype(dtype).astype(np.float64)
    return np.moveaxis((codes * scale).reshape(v.shape), -1, axis)


WIDE = False


def mx_kscale(k):
    if not WIDE:
        return np.ones(k)
    levels = np.array([10, -10, 5, -5, 0])
    if k % 512:
        return np.exp2(np.random.permutation(np.resize(levels, k // 32))).repeat(32)
    a = np.empty((k // 512, 16))
    for p in range(k // 512):
        a[p, :8] = np.random.permutation(np.resize(levels, 8))
        for g in range(8):
            far = levels[np.abs(levels - a[p, g]) >= 10]
            a[p, g + 8] = far[np.random.randint(len(far))]
    return np.exp2(a.ravel()).repeat(32)


def f64(x):
    return np.asarray(x).astype(np.float64)


def striped(idx):
    return np.tile(idx.reshape(-1, 16).T, (8, 1)).astype(np.uint16)


def unstriped(offs):
    return offs[:16].T.reshape(-1).astype(np.int64)


E2M1 = np.array([0.0, 0.5, 1.0, 1.5, 2.0, 3.0, 4.0, 6.0, -0.0, -0.5, -1.0, -1.5, -2.0, -3.0, -4.0, -6.0])


def pack_weight(w, fmt):
    k, n = w.shape
    w = f64(np.asarray(w, np.float32).astype(ml_dtypes.bfloat16)).reshape(k // 32, 32, n)
    amax = np.abs(w).max(1)
    if fmt == "e4m3":
        byte = np.frexp(amax)[1] - 1 + 127 - 7
    else:
        mant, ex = np.frexp(amax / 6.0)
        byte = np.where(mant > 0.5, ex, ex - 1) + 127
    byte = np.clip(np.where(amax > 0, byte, 1), 1, 254)
    scaled = (w * np.exp2(127.0 - byte)[:, None, :]).reshape(k, n).astype(np.float32)
    by_word = np.ascontiguousarray(scaled.reshape(k // 512, 128, 4, n).transpose(0, 1, 3, 2))
    if fmt == "e4m3":
        words = by_word.astype(ml_dtypes.float8_e4m3fn).view(np.uint8)
    else:
        c = by_word.astype(ml_dtypes.float4_e2m1fn).view(np.uint8) & 0xF
        words = (c[..., 0::2] | (c[..., 1::2] << 4)).reshape(k // 512, 128, 2 * n)
    return np.ascontiguousarray(words), np.ascontiguousarray(byte.astype(np.uint8).reshape(k // 512, 16, n))


def unpack_weight(words, scales, fmt):
    g, _, n = scales.shape
    words = np.ascontiguousarray(words).reshape(g, 128, n, -1)
    if fmt == "e4m3":
        vals = words.view(ml_dtypes.float8_e4m3fn).astype(np.float64)
    else:
        nib = np.empty((g, 128, n, 4), np.uint8)
        nib[..., 0::2] = words & 0xF
        nib[..., 1::2] = words >> 4
        vals = E2M1[nib]
    vals = vals * np.repeat(np.exp2(scales.astype(np.float64) - 127.0), 8, axis=1)[..., None]
    return vals.transpose(0, 1, 3, 2).reshape(g * 512, n)


def gelu(v):
    return 0.5 * v * (1.0 + np.tanh(np.sqrt(2.0 / np.pi) * (v + 0.044715 * v**3)))


def bf(x):
    return np.asarray(x, np.float32).astype(ml_dtypes.bfloat16)


def planes(Y):
    n, m = Y.shape
    b = f64(bf(Y)).reshape(n // 32, 32, m)
    amax = np.abs(b).max(1)
    byte = np.clip(np.where(amax > 0, np.frexp(amax)[1] - 1 + 127 - 7, 1), 1, 254)
    codes = (b * np.exp2(127.0 - byte)[:, None, :]).reshape(n, m).astype(np.float32).astype(ml_dtypes.float8_e4m3fn).view(np.uint8)
    words = codes.reshape(n // 512, 128, 4, m).transpose(0, 1, 3, 2)
    return np.ascontiguousarray(words), np.ascontiguousarray(byte.astype(np.uint8).reshape(n // 512, 16, m))


K, T, S, H, T2, P, N = 512, 4096, 1024, 1024, 2048, 512, 768


def setup_inputs():
    n = np.random.standard_normal
    s = mx_kscale(K)[:, None]
    u = mx_kscale(H)[:, None]
    d = {}
    d["tab_words"], d["tab_scales"] = pack_weight(n((K, T)) * s, "e4m3")
    d["offs"] = striped(np.random.permutation(T)[:S])
    d["w1"] = (n((K, H)) / K**0.5 / s * u.T).astype(np.float32)
    d["w4_words"], d["w4_scales"] = pack_weight(n((K, H)) / K**0.5 / s * u.T, "e2m1")
    d["thr"] = (0.5 * n(H) * u[:, 0]).astype(np.float32)
    d["wgs"] = np.exp(0.3 * n((128, S))).astype(np.float32)
    d["page0"] = (n((H, T2)) * u).astype(np.float32)
    d["offs2"] = striped(np.random.permutation(T2)[:S])
    d["offs3"] = striped(np.random.permutation(T2)[:P])
    d["b2"] = (0.5 * n(H) * u[:, 0]).astype(np.float32)
    d["w2"] = (0.42 * n((H, N)) / H**0.5 / u).astype(np.float32)
    return d


def reference(tab_words, tab_scales, offs, w1, w4_words, w4_scales, thr, wgs, page0, offs2, offs3, b2, w2):
    v = unpack_weight(tab_words, tab_scales, "e4m3")[:, unstriped(offs)]
    w4 = unpack_weight(w4_words, w4_scales, "e2m1")
    left = mxq(f64(w1), 0, "e4m3").T @ v
    right = w4.T @ v
    h = np.minimum(left, right) - f64(thr)[:, None]
    page = f64(page0).copy()
    page[:, unstriped(offs2)] = np.tile(f64(wgs), (H // 128, 1)) * h
    x = page[:, unstriped(offs3)] + f64(b2)[:, None]
    tone = mxq(f64(w2), 0, "e4m3").T @ mxq(x, 0, "e4m3")
    y = tone * np.cos(tone)
    words, scales = planes(page)
    return y, page, words, scales

@@ -1,0 +1,311 @@
+import math
+from contextlib import ExitStack
+
+import concourse.mybir as mybir
+
+K, T, S, H, T2, M, N = 512, 4096, 1024, 1024, 2048, 512, 768
+FLOPS = 2 * (2 * K * H * S + H * N * M)
+
+F32 = mybir.dt.float32
+BF16 = mybir.dt.bfloat16
+I32 = mybir.dt.int32
+U32 = mybir.dt.uint32
+U16 = mybir.dt.uint16
+U8 = mybir.dt.uint8
+FP8X4 = mybir.dt.float8_e4m3fn_x4
+FP4X4 = mybir.dt.float4_e2m1fn_x4
+ALU = mybir.AluOpType
+ACT = mybir.ActivationFunctionType
+
+P = 128
+PACK = 4
+PASS = P * PACK
+GROUPS = H // PASS
+SLICES = GROUPS * PACK
+BANK = 512
+HALVES = S // BANK
+QUADS = 4
+CHUNK = 512
+CHUNKS = T2 // CHUNK
+TILES = N // P
+
+
+def tile_list_masking_tone_page_kernel(
+    tc, tab_words, tab_scales, offs, w1, w4_words, w4_scales, thr, wgs, page0, offs2, offs3, b2, w2,
+    out_0, out_1, out_2, out_3,
+):
+    nc = tc.nc
+    with ExitStack() as ctx:
+        lists = ctx.enter_context(tc.tile_pool(name="lists", bufs=1))
+        keep = ctx.enter_context(tc.tile_pool(name="keep", bufs=1))
+        psum = ctx.enter_context(tc.psum_pool(name="psum", bufs=1))
+
+        idx = lists.tile([P, S // 16], U16, name="idx")
+        idx2 = lists.tile([P, S // 16], U16, name="idx2")
+        idx3 = lists.tile([P, M // 16], U16, name="idx3")
+
+        tab_s = keep.tile([P, T], U8, name="tab_s", tag="tab_s", align_bytes=64)
+        w4_s_raw = keep.tile([P, H], U8, name="w4_s_raw", tag="woven2", align_bytes=64)
+        nc.vector.memset(tab_s[:].bitcast(I32), 0)
+        nc.vector.memset(w4_s_raw[:].bitcast(I32), 0)
+
+        warm = keep.tile([P, 2], F32, name="warm")
+        nc.gpsimd.memset(warm[:, 0:1], 0.0)
+        nc.scalar.activation(out=warm[:, 1:2], in_=warm[:, 0:1], func=ACT.Sin, scale=0.5)
+        for q in range(QUADS):
+            nc.gpsimd.dma_start(
+                out=tab_s[32 * q : 32 * q + 4, :].bitcast(I32),
+                in_=tab_scales[0, 4 * q : 4 * q + 4, :].bitcast(I32),
+            )
+        for q in range(QUADS):
+            nc.gpsimd.dma_start(
+                out=w4_s_raw[32 * q : 32 * q + 4, :].bitcast(I32),
+                in_=w4_scales[0, 4 * q : 4 * q + 4, :].bitcast(I32),
+            )
+
+        w1_rows = w1.rearrange("(p j) (g c) -> g p j c", j=PACK, c=PASS)
+        w2_rows = w2.rearrange("(g p j) n -> g p j n", p=P, j=PACK)
+        page_rows = page0.rearrange("(g p t) c -> g t p c", p=P, t=PACK)
+        out_rows = out_1.rearrange("(g p t) c -> g t p c", p=P, t=PACK)
+        wgs_rows = wgs.rearrange("(q t) j -> q t j", t=PACK)
+
+        thr_t = keep.tile([P, GROUPS, PACK], F32, name="thr_t")
+        b2_t = keep.tile([P, GROUPS, PACK], F32, name="b2_t")
+        w4_raw = keep.tile([P, 2 * H], U8, name="w4_raw", tag="woven1", align_bytes=64)
+        w1_raw = [
+            keep.tile([P, PACK, PASS], F32, name="w1_raw0", tag="rawB"),
+            keep.tile([P, PACK, PASS], F32, name="w1_raw1", tag="rawC"),
+        ]
+        tab_w = keep.tile([P, T], U32, name="tab_w", tag="rawA")
+        wg_first = keep.tile([P, S], F32, name="wg_first")
+        wg_rest = keep.tile([P, PACK - 1, S], F32, name="wg_rest")
+        pages = [keep.tile([P, T2], F32, name="page%d" % s) for s in range(SLICES)]
+
+        nc.sync.dma_start(out=idx[:], in_=offs)
+        nc.sync.dma_start(out=w4_raw[:].bitcast(I32), in_=w4_words[0].bitcast(I32))
+        nc.sync.dma_start(out=w1_raw[0][:], in_=w1_rows[0])
+        nc.sync.dma_start(out=thr_t[:], in_=thr.rearrange("(g p t) -> p g t", p=P, t=PACK))
+        nc.sync.dma_start(
+            out=tab_w[:].bitcast(I32), in_=tab_words[0].rearrange("p c i -> p (c i)").bitcast(I32)
+        )
+        nc.sync.dma_start(out=idx2[:], in_=offs2)
+        for q in range(QUADS):
+            nc.sync.dma_start(out=wg_first[32 * q : 32 * q + 32, :], in_=wgs_rows[:, 0, :])
+        nc.sync.dma_start(out=pages[0][:], in_=page_rows[0, 0])
+        nc.sync.dma_start(out=idx3[:], in_=offs3)
+        nc.sync.dma_start(out=b2_t[:], in_=b2.rearrange("(g p t) -> p g t", p=P, t=PACK))
+        for q in range(QUADS):
+            nc.sync.dma_start(out=wg_rest[32 * q : 32 * q + 32, :, :], in_=wgs_rows[:, 1:PACK, :])
+        nc.sync.dma_start(out=pages[1][:], in_=page_rows[0, 1])
+        nc.sync.dma_start(out=w1_raw[1][:], in_=w1_rows[1])
+        nc.sync.dma_start(out=pages[2][:], in_=page_rows[0, 2])
+
+        neg_thr = keep.tile([P, GROUPS, PACK], F32, name="neg_thr")
+        nc.scalar.mul(neg_thr[:], thr_t[:], -1.0)
+
+        w4_c = keep.tile([P, 2 * H], U8, name="w4_c", align_bytes=64)
+        w4_s = keep.tile([P, H], U8, name="w4_s", align_bytes=64)
+        nc.vector.tensor_copy(
+            out=w4_c[:].rearrange("p (g t m e) -> p g m t e", g=GROUPS, t=PACK, e=2),
+            in_=w4_raw[:].rearrange("p (g m t e) -> p g m t e", g=GROUPS, t=PACK, e=2),
+        )
+        nc.vector.tensor_copy(
+            out=w4_s[:].rearrange("p (g t m) -> p g m t", g=GROUPS, t=PACK),
+            in_=w4_s_raw[:].rearrange("p (g m t) -> p g m t", g=GROUPS, t=PACK),
+        )
+
+        w1_c = [keep.tile([P, PASS], U32, name="w1_c%d" % g, align_bytes=64) for g in range(GROUPS)]
+        w1_s = [keep.tile([P, PASS], U8, name="w1_s%d" % g, align_bytes=64) for g in range(GROUPS)]
+
+        def quantize_w1(g):
+            grouped = keep.tile([P, PACK * PASS], BF16, name="w1_bf%d" % g, tag="wbf%d" % g, align_bytes=64)
+            nc.scalar.copy(
+                out=grouped[:].rearrange("p (t m j) -> p m j t", t=PACK, j=PACK),
+                in_=w1_raw[g][:].rearrange("p j (m t) -> p m j t", t=PACK),
+            )
+            nc.vector.quantize_mx(out=w1_c[g][:].bitcast(FP8X4), scales=w1_s[g][:], in_=grouped[:])
+
+        v_s = keep.tile([P, S], U8, name="v_s", align_bytes=64)
+        nc.vector.tensor_copy(out=v_s[:], in_=tab_s[:].indirect(idx[:]))
+        quantize_w1(0)
+        v_c = [
+            keep.tile([P, BANK], U32, name="v_c0", tag="tab_s", align_bytes=64),
+            keep.tile([P, BANK], U32, name="v_c1", align_bytes=64),
+        ]
+        for u in range(HALVES):
+            cols = BANK // 16
+            nc.vector.tensor_copy(out=v_c[u][:], in_=tab_w[:].indirect(idx[:, u * cols : (u + 1) * cols]))
+
+        w2_raw = [
+            keep.tile([P, PACK, N], F32, name="w2_raw0", tag="rawB"),
+            keep.tile([P, PACK, N], F32, name="w2_raw1", tag="rawA"),
+        ]
+        nc.sync.dma_start(out=w2_raw[0][:], in_=w2_rows[0])
+        nc.sync.dma_start(out=pages[3][:], in_=page_rows[0, 3])
+        nc.sync.dma_start(out=w2_raw[1][:], in_=w2_rows[1])
+        for t in range(PACK):
+            nc.sync.dma_start(out=pages[PACK + t][:], in_=page_rows[1, t])
+
+        w2_c = [keep.tile([P, N], U32, name="w2_c%d" % g, align_bytes=64) for g in range(GROUPS)]
+        w2_s = [keep.tile([P, N], U8, name="w2_s%d" % g, align_bytes=64) for g in range(GROUPS)]
+
+        def quantize_w2(g):
+            grouped = keep.tile([P, PACK * N], BF16, name="w2_bf%d" % g, tag="wbf%d" % g, align_bytes=64)
+            for lo, hi in ((0, 512), (512, N)):
+                nc.scalar.copy(
+                    out=grouped[:, PACK * lo : PACK * hi].rearrange("p (c i j) -> p c j i", i=4, j=PACK),
+                    in_=w2_raw[g][:, :, lo:hi].rearrange("p j (c i) -> p c j i", i=4),
+                )
+                nc.vector.quantize_mx(
+                    out=w2_c[g][:, lo:hi].bitcast(FP8X4),
+                    scales=w2_s[g][:, lo:hi],
+                    in_=grouped[:, PACK * lo : PACK * hi],
+                )
+
+        h_tiles = {}
+        x_bf = [keep.tile([P, M, PACK], BF16, name="x_bf%d" % g, align_bytes=64) for g in range(GROUPS)]
+        x_c = [keep.tile([P, M], U32, name="x_c%d" % g, align_bytes=64) for g in range(GROUPS)]
+        x_s = [keep.tile([P, M], U8, name="x_s%d" % g, align_bytes=64) for g in range(GROUPS)]
+
+        def make_h(s):
+            g, t = divmod(s, PACK)
+            cols = slice(t * P, (t + 1) * P)
+            c4 = g * PASS + t * P
+            h = keep.tile([P, S], F32, name="h%d" % s, tag="h%d" % (s % 2), align_bytes=64)
+            h_tiles[s] = h
+            lefts, rights, lows = [], [], []
+            for u in range(HALVES):
+                left = psum.tile([P, BANK], F32, name="left%d_%d" % (s, u), tag="bank%d" % u)
+                nc.tensor.matmul_mx(
+                    out=left[:], lhsT=w1_c[g][:, cols].bitcast(FP8X4), lhsT_scale=w1_s[g][:, cols],
+                    rhs=v_c[u][:].bitcast(FP8X4), rhs_scale=v_s[:, u * BANK : (u + 1) * BANK],
+                    start=True, stop=True,
+                )
+                low = keep.tile([P, BANK], F32, name="low%d_%d" % (s, u), tag="low%d" % u)
+                nc.scalar.activation(
+                    out=low[:], in_=left[:], func=ACT.Identity, bias=neg_thr[:, g, t : t + 1], scale=1.0
+                )
+                lows.append(low)
+            for u in range(HALVES):
+                right = psum.tile([P, BANK], F32, name="right%d_%d" % (s, u), tag="bank%d" % (HALVES + u))
+                nc.tensor.matmul_mx(
+                    out=right[:], lhsT=w4_c[:, 2 * c4 : 2 * (c4 + P)].bitcast(FP4X4),
+                    lhsT_scale=w4_s[:, c4 : c4 + P],
+                    rhs=v_c[u][:].bitcast(FP8X4), rhs_scale=v_s[:, u * BANK : (u + 1) * BANK],
+                    start=True, stop=True,
+                )
+                nc.vector.scalar_tensor_tensor(
+                    out=h[:, u * BANK : (u + 1) * BANK], in0=right[:], scalar=neg_thr[:, g, t : t + 1],
+                    in1=lows[u][:], op0=ALU.add, op1=ALU.min,
+                )
+
+        def scatter(s):
+            g, t = divmod(s, PACK)
+            wg = wg_first[:] if t == 0 else wg_rest[:, t - 1, :]
+            nc.vector.tensor_tensor(out=pages[s][:].indirect(idx2[:]), in0=h_tiles[s][:], in1=wg, op=ALU.mult)
+            nc.sync.dma_start(out=out_rows[g, t], in_=pages[s][:])
+
+        def pick(s):
+            g, t = divmod(s, PACK)
+            picked = keep.tile([P, M], F32, name="picked%d" % s, tag="low0")
+            nc.vector.tensor_copy(out=picked[:], in_=pages[s][:].indirect(idx3[:]))
+            nc.scalar.activation(
+                out=x_bf[g][:, :, t], in_=picked[:], func=ACT.Identity, bias=b2_t[:, g, t : t + 1], scale=1.0
+            )
+            if t == PACK - 1:
+                nc.vector.quantize_mx(
+                    out=x_c[g][:].bitcast(FP8X4), scales=x_s[g][:], in_=x_bf[g][:].rearrange("p m t -> p (m t)")
+                )
+
+        pairs = {}
+        woven = {}
+
+        def round_page(s):
+            g, t = divmod(s, PACK)
+            for c in range(CHUNKS):
+                if t == 0:
+                    pairs[g, c] = keep.tile([P, 2, CHUNK, 2], BF16, name="pairs%d_%d" % (g, c), tag="pairs%d" % c)
+                nc.scalar.copy(out=pairs[g, c][:, t // 2, :, t % 2], in_=pages[s][:, c * CHUNK : (c + 1) * CHUNK])
+
+        def weave(g, c, copy):
+            tile = keep.tile([P, CHUNK * PACK], BF16, name="woven%d_%d" % (g, c), tag="woven%d" % c, align_bytes=64)
+            woven[g, c] = tile
+            words = pairs[g, c][:].rearrange("p u m e -> p (u m e)").bitcast(F32)
+            copy(
+                out=tile[:].bitcast(F32).rearrange("p (a i u) -> p a u i", i=4, u=2),
+                in_=words.rearrange("p (u a i) -> p a u i", i=4, u=2),
+            )
+
+        planes = {}
+
+        def quantize_page(g, c):
+            if c == 0:
+                planes[g] = (
+                    keep.tile([P, T2], U32, name="page_c%d" % g, tag="h%d" % g, align_bytes=64),
+                    keep.tile([P, T2], U8, name="page_s%d" % g, align_bytes=64),
+                )
+            codes, scales = planes[g]
+            words = out_2[g].rearrange("p c i -> p (c i)").bitcast(I32)
+            cols = slice(c * CHUNK, (c + 1) * CHUNK)
+            nc.vector.quantize_mx(out=codes[:, cols].bitcast(FP8X4), scales=scales[:, cols], in_=woven[g, c][:])
+            nc.sync.dma_start(out=words[:, cols], in_=codes[:, cols].bitcast(I32))
+            if c == CHUNKS - 1:
+                for q in range(QUADS):
+                    nc.sync.dma_start(
+                        out=out_3[g, 4 * q : 4 * q + 4, :].bitcast(I32),
+                        in_=scales[32 * q : 32 * q + 4, :].bitcast(I32),
+                    )
+
+        tones = {}
+
+        def tone_pass(g, n):
+            if g == 0:
+                tones[n] = psum.tile([P, M], F32, name="tone%d" % n, tag="bank%d" % ((2 * HALVES + n) % 8))
+            cols = slice(n * P, (n + 1) * P)
+            nc.tensor.matmul_mx(
+                out=tones[n][:], lhsT=w2_c[g][:, cols].bitcast(FP8X4), lhsT_scale=w2_s[g][:, cols],
+                rhs=x_c[g][:].bitcast(FP8X4), rhs_scale=x_s[g][:], start=(g == 0), stop=(g == GROUPS - 1),
+            )
+
+        def finish(n):
+            size = keep.tile([P, M], F32, name="size%d" % n, tag="size", bufs=2)
+            nc.scalar.activation(out=size[:], in_=tones[n][:], func=ACT.Abs)
+            cosine = keep.tile([P, M], F32, name="cosine%d" % n, tag="cosine", bufs=2)
+            nc.scalar.activation(out=cosine[:], in_=size[:], func=ACT.Sin, scale=-1.0, bias=math.pi / 2)
+            y = keep.tile([P, M], F32, name="y%d" % n, tag="y", bufs=3)
+            nc.vector.tensor_tensor(out=y[:], in0=tones[n][:], in1=cosine[:], op=ALU.mult)
+            nc.sync.dma_start(out=out_0[n * P : (n + 1) * P, :], in_=y[:])
+
+        make_h(0)
+        for s in range(SLICES):
+            scatter(s)
+            if s + 1 < SLICES:
+                make_h(s + 1)
+            pick(s)
+            if s == 1:
+                quantize_w1(1)
+            if s in (2, 3):
+                quantize_w2(s - 2)
+            if s == 5:
+                for n in range(4):
+                    tone_pass(0, n)
+            if s == 6:
+                for n in range(4, TILES):
+                    tone_pass(0, n)
+                for c in range(CHUNKS):
+                    quantize_page(0, c)
+            if 1 <= s < SLICES - 1:
+                round_page(s - 1)
+            if s == PACK:
+                for c in range(CHUNKS):
+                    weave(0, c, nc.scalar.copy)
+            if s == SLICES - 2:
+                round_page(s)
+        for n in range(TILES):
+            tone_pass(1, n)
+        round_page(SLICES - 1)
+        for n in range(TILES):
+            finish(n)
+            if n < CHUNKS:
+                weave(1, n, nc.vector.tensor_copy)
+                quantize_page(1, n)

@@ -28,6 +28,7 @@ QUADS = 4
 CHUNK = 512
 CHUNKS = T2 // CHUNK
 TILES = N // P
+PAGE_SLOTS = ("page0", "page1", "page2", "page3", "low00", "low10", "picked0", "w1_raw")
 
 
 def tile_list_masking_tone_page_kernel(
@@ -44,64 +45,57 @@ def tile_list_masking_tone_page_kernel(
         idx2 = lists.tile([P, S // 16], U16, name="idx2")
         idx3 = lists.tile([P, M // 16], U16, name="idx3")
 
-        tab_s = keep.tile([P, T], U8, name="tab_s", tag="tab_s", align_bytes=64)
-        w4_s_raw = keep.tile([P, H], U8, name="w4_s_raw", tag="woven2", align_bytes=64)
+        tab_s = keep.tile([P, T], U8, name="tab_s", tag="page2", align_bytes=64)
+        w4_s_raw = keep.tile([P, H], U8, name="w4_s_raw", tag="wg_first", align_bytes=64)
         nc.vector.memset(tab_s[:].bitcast(I32), 0)
-        nc.vector.memset(w4_s_raw[:].bitcast(I32), 0)
 
-        warm = keep.tile([P, 2], F32, name="warm")
-        nc.gpsimd.memset(warm[:, 0:1], 0.0)
-        nc.scalar.activation(out=warm[:, 1:2], in_=warm[:, 0:1], func=ACT.Sin, scale=0.5)
-        for q in range(QUADS):
-            nc.gpsimd.dma_start(
-                out=tab_s[32 * q : 32 * q + 4, :].bitcast(I32),
-                in_=tab_scales[0, 4 * q : 4 * q + 4, :].bitcast(I32),
-            )
-        for q in range(QUADS):
-            nc.gpsimd.dma_start(
-                out=w4_s_raw[32 * q : 32 * q + 4, :].bitcast(I32),
-                in_=w4_scales[0, 4 * q : 4 * q + 4, :].bitcast(I32),
-            )
-
+        warm_in = keep.tile([P, 1], F32, name="warm_in", tag="page3", align_bytes=64)
+        warm_out = keep.tile([P, 1], F32, name="warm_out", tag="page0", align_bytes=64)
+        nc.gpsimd.memset(warm_in[:], 0.0)
+        nc.scalar.activation(out=warm_out[:], in_=warm_in[:], func=ACT.Sin)
         w1_rows = w1.rearrange("(p j) (g c) -> g p j c", j=PACK, c=PASS)
         w2_rows = w2.rearrange("(g p j) n -> g p j n", p=P, j=PACK)
         page_rows = page0.rearrange("(g p t) c -> g t p c", p=P, t=PACK)
         out_rows = out_1.rearrange("(g p t) c -> g t p c", p=P, t=PACK)
         wgs_rows = wgs.rearrange("(q t) j -> q t j", t=PACK)
 
-        thr_t = keep.tile([P, GROUPS, PACK], F32, name="thr_t")
-        b2_t = keep.tile([P, GROUPS, PACK], F32, name="b2_t")
-        w4_raw = keep.tile([P, 2 * H], U8, name="w4_raw", tag="woven1", align_bytes=64)
-        w1_raw = [
-            keep.tile([P, PACK, PASS], F32, name="w1_raw0", tag="rawB"),
-            keep.tile([P, PACK, PASS], F32, name="w1_raw1", tag="rawC"),
-        ]
-        tab_w = keep.tile([P, T], U32, name="tab_w", tag="rawA")
-        wg_first = keep.tile([P, S], F32, name="wg_first")
-        wg_rest = keep.tile([P, PACK - 1, S], F32, name="wg_rest")
-        pages = [keep.tile([P, T2], F32, name="page%d" % s) for s in range(SLICES)]
+        thr_t = keep.tile([P, GROUPS, PACK], F32, name="thr_t", tag="thr_t")
+        w4_raw = keep.tile([P, 2 * H], U8, name="w4_raw", tag="wg_rest", align_bytes=64)
+        tab_w = keep.tile([P, T], U32, name="tab_w", tag="page3", align_bytes=64)
+        w1_raw = {0: keep.tile([P, PACK, PASS], F32, name="w1_raw0", tag="w1_raw", align_bytes=64)}
 
         nc.sync.dma_start(out=idx[:], in_=offs)
-        nc.sync.dma_start(out=w4_raw[:].bitcast(I32), in_=w4_words[0].bitcast(I32))
+        nc.sync.dma_start(out=idx2[:], in_=offs2)
+        nc.sync.dma_start(out=idx3[:], in_=offs3)
+        for q in range(QUADS):
+            nc.sync.dma_start(
+                out=w4_s_raw[32 * q : 32 * q + 32, :].bitcast(I32),
+                in_=w4_scales[0, 4 * q : 4 * q + 4, :].bitcast(I32).unsqueeze(0).broadcast_to([8, 4, H // 4]),
+            )
         nc.sync.dma_start(out=w1_raw[0][:], in_=w1_rows[0])
+        nc.sync.dma_start(out=w4_raw[:].bitcast(I32), in_=w4_words[0].bitcast(I32))
         nc.sync.dma_start(out=thr_t[:], in_=thr.rearrange("(g p t) -> p g t", p=P, t=PACK))
+        for q in range(QUADS):
+            nc.sync.dma_start(
+                out=tab_s[32 * q : 32 * q + 4, :].bitcast(I32),
+                in_=tab_scales[0, 4 * q : 4 * q + 4, :].bitcast(I32),
+            )
         nc.sync.dma_start(
             out=tab_w[:].bitcast(I32), in_=tab_words[0].rearrange("p c i -> p (c i)").bitcast(I32)
         )
-        nc.sync.dma_start(out=idx2[:], in_=offs2)
-        for q in range(QUADS):
-            nc.sync.dma_start(out=wg_first[32 * q : 32 * q + 32, :], in_=wgs_rows[:, 0, :])
-        nc.sync.dma_start(out=pages[0][:], in_=page_rows[0, 0])
-        nc.sync.dma_start(out=idx3[:], in_=offs3)
-        nc.sync.dma_start(out=b2_t[:], in_=b2.rearrange("(g p t) -> p g t", p=P, t=PACK))
-        for q in range(QUADS):
-            nc.sync.dma_start(out=wg_rest[32 * q : 32 * q + 32, :, :], in_=wgs_rows[:, 1:PACK, :])
-        nc.sync.dma_start(out=pages[1][:], in_=page_rows[0, 1])
-        nc.sync.dma_start(out=w1_raw[1][:], in_=w1_rows[1])
-        nc.sync.dma_start(out=pages[2][:], in_=page_rows[0, 2])
+
+        pages = {}
+
+        def load_page(s):
+            pages[s] = keep.tile([P, T2], F32, name="page%d" % s, tag=PAGE_SLOTS[s], align_bytes=64)
+            nc.sync.dma_start(out=pages[s][:], in_=page_rows[s // PACK, s % PACK])
+
+        load_page(0)
 
         neg_thr = keep.tile([P, GROUPS, PACK], F32, name="neg_thr")
-        nc.scalar.mul(neg_thr[:], thr_t[:], -1.0)
+        nc.gpsimd.tensor_scalar(
+            out=neg_thr[:], in0=thr_t[:], scalar1=-1.0, scalar2=0.0, op0=ALU.mult, op1=ALU.add
+        )
 
         w4_c = keep.tile([P, 2 * H], U8, name="w4_c", align_bytes=64)
         w4_s = keep.tile([P, H], U8, name="w4_s", align_bytes=64)
@@ -114,11 +108,15 @@ def tile_list_masking_tone_page_kernel(
             in_=w4_s_raw[:].rearrange("p (g m t) -> p g m t", g=GROUPS, t=PACK),
         )
 
+        wg_first = keep.tile([P, S], F32, name="wg_first", tag="wg_first", align_bytes=64)
+        for q in range(QUADS):
+            nc.sync.dma_start(out=wg_first[32 * q : 32 * q + 32, :], in_=wgs_rows[:, 0, :])
+
         w1_c = [keep.tile([P, PASS], U32, name="w1_c%d" % g, align_bytes=64) for g in range(GROUPS)]
         w1_s = [keep.tile([P, PASS], U8, name="w1_s%d" % g, align_bytes=64) for g in range(GROUPS)]
 
         def quantize_w1(g):
-            grouped = keep.tile([P, PACK * PASS], BF16, name="w1_bf%d" % g, tag="wbf%d" % g, align_bytes=64)
+            grouped = keep.tile([P, PACK * PASS], BF16, name="w1_bf%d" % g, tag=("page1", "w1_bf1")[g], align_bytes=64)
             nc.scalar.copy(
                 out=grouped[:].rearrange("p (t m j) -> p m j t", t=PACK, j=PACK),
                 in_=w1_raw[g][:].rearrange("p j (m t) -> p m j t", t=PACK),
@@ -129,37 +127,45 @@ def tile_list_masking_tone_page_kernel(
         nc.vector.tensor_copy(out=v_s[:], in_=tab_s[:].indirect(idx[:]))
         quantize_w1(0)
         v_c = [
-            keep.tile([P, BANK], U32, name="v_c0", tag="tab_s", align_bytes=64),
+            keep.tile([P, BANK], U32, name="v_c0", align_bytes=64),
             keep.tile([P, BANK], U32, name="v_c1", align_bytes=64),
         ]
         for u in range(HALVES):
             cols = BANK // 16
             nc.vector.tensor_copy(out=v_c[u][:], in_=tab_w[:].indirect(idx[:, u * cols : (u + 1) * cols]))
 
-        w2_raw = [
-            keep.tile([P, PACK, N], F32, name="w2_raw0", tag="rawB"),
-            keep.tile([P, PACK, N], F32, name="w2_raw1", tag="rawA"),
-        ]
-        nc.sync.dma_start(out=w2_raw[0][:], in_=w2_rows[0])
-        nc.sync.dma_start(out=pages[3][:], in_=page_rows[0, 3])
-        nc.sync.dma_start(out=w2_raw[1][:], in_=w2_rows[1])
-        for t in range(PACK):
-            nc.sync.dma_start(out=pages[PACK + t][:], in_=page_rows[1, t])
+        wg_rest = keep.tile([P, PACK - 1, S], F32, name="wg_rest", tag="wg_rest", align_bytes=64)
+        for q in range(QUADS):
+            nc.sync.dma_start(out=wg_rest[32 * q : 32 * q + 32, :, :], in_=wgs_rows[:, 1:PACK, :])
+        load_page(1)
+        b2_t = keep.tile([P, GROUPS, PACK], F32, name="b2_t", tag="thr_t")
+        nc.sync.dma_start(out=b2_t[:], in_=b2.rearrange("(g p t) -> p g t", p=P, t=PACK))
+        w1_raw[1] = keep.tile([P, PACK, PASS], F32, name="w1_raw1", tag="w1_raw", align_bytes=64)
+        nc.sync.dma_start(out=w1_raw[1][:], in_=w1_rows[1])
+        load_page(2)
+        load_page(3)
 
         w2_c = [keep.tile([P, N], U32, name="w2_c%d" % g, align_bytes=64) for g in range(GROUPS)]
         w2_s = [keep.tile([P, N], U8, name="w2_s%d" % g, align_bytes=64) for g in range(GROUPS)]
 
-        def quantize_w2(g):
-            grouped = keep.tile([P, PACK * N], BF16, name="w2_bf%d" % g, tag="wbf%d" % g, align_bytes=64)
-            for lo, hi in ((0, 512), (512, N)):
+        w2_raw = {}
+
+        def load_w2(g):
+            w2_raw[g] = keep.tile([P, PACK, N], F32, name="w2_raw%d" % g, tag="low%d1" % g, align_bytes=64)
+            nc.sync.dma_start(out=w2_raw[g][:], in_=w2_rows[g])
+
+        def quantize_w2(g, part):
+            raw = w2_raw[g]
+            for lo, hi in (((0, 512), (512, N))[part],):
+                grouped = keep.tile([P, PACK * (hi - lo)], BF16, name="w2_bf%d_%d" % (g, part), tag="w2_bf%d" % part, align_bytes=64)
                 nc.scalar.copy(
-                    out=grouped[:, PACK * lo : PACK * hi].rearrange("p (c i j) -> p c j i", i=4, j=PACK),
-                    in_=w2_raw[g][:, :, lo:hi].rearrange("p j (c i) -> p c j i", i=4),
+                    out=grouped[:].rearrange("p (c i j) -> p c j i", i=4, j=PACK),
+                    in_=raw[:, :, lo:hi].rearrange("p j (c i) -> p c j i", i=4),
                 )
                 nc.vector.quantize_mx(
                     out=w2_c[g][:, lo:hi].bitcast(FP8X4),
                     scales=w2_s[g][:, lo:hi],
-                    in_=grouped[:, PACK * lo : PACK * hi],
+                    in_=grouped[:],
                 )
 
         h_tiles = {}
@@ -171,32 +177,31 @@ def tile_list_masking_tone_page_kernel(
             g, t = divmod(s, PACK)
             cols = slice(t * P, (t + 1) * P)
             c4 = g * PASS + t * P
-            h = keep.tile([P, S], F32, name="h%d" % s, tag="h%d" % (s % 2), align_bytes=64)
+            h = keep.tile([P, S], F32, name="h%d" % s, tag="h")
             h_tiles[s] = h
-            lefts, rights, lows = [], [], []
             for u in range(HALVES):
+                half = slice(u * BANK, (u + 1) * BANK)
                 left = psum.tile([P, BANK], F32, name="left%d_%d" % (s, u), tag="bank%d" % u)
                 nc.tensor.matmul_mx(
                     out=left[:], lhsT=w1_c[g][:, cols].bitcast(FP8X4), lhsT_scale=w1_s[g][:, cols],
-                    rhs=v_c[u][:].bitcast(FP8X4), rhs_scale=v_s[:, u * BANK : (u + 1) * BANK],
-                    start=True, stop=True,
+                    rhs=v_c[u][:].bitcast(FP8X4), rhs_scale=v_s[:, half], start=True, stop=True,
                 )
-                low = keep.tile([P, BANK], F32, name="low%d_%d" % (s, u), tag="low%d" % u)
+                low = keep.tile(
+                    [P, BANK], F32, name="low%d_%d" % (s, u),
+                    tag=("low%d" % u if s > 1 else "low%d%d" % (s, u)), align_bytes=64,
+                )
                 nc.scalar.activation(
                     out=low[:], in_=left[:], func=ACT.Identity, bias=neg_thr[:, g, t : t + 1], scale=1.0
                 )
-                lows.append(low)
-            for u in range(HALVES):
                 right = psum.tile([P, BANK], F32, name="right%d_%d" % (s, u), tag="bank%d" % (HALVES + u))
                 nc.tensor.matmul_mx(
                     out=right[:], lhsT=w4_c[:, 2 * c4 : 2 * (c4 + P)].bitcast(FP4X4),
                     lhsT_scale=w4_s[:, c4 : c4 + P],
-                    rhs=v_c[u][:].bitcast(FP8X4), rhs_scale=v_s[:, u * BANK : (u + 1) * BANK],
-                    start=True, stop=True,
+                    rhs=v_c[u][:].bitcast(FP8X4), rhs_scale=v_s[:, half], start=True, stop=True,
                 )
                 nc.vector.scalar_tensor_tensor(
-                    out=h[:, u * BANK : (u + 1) * BANK], in0=right[:], scalar=neg_thr[:, g, t : t + 1],
-                    in1=lows[u][:], op0=ALU.add, op1=ALU.min,
+                    out=h[:, half], in0=right[:], scalar=neg_thr[:, g, t : t + 1],
+                    in1=low[:], op0=ALU.add, op1=ALU.min,
                 )
 
         def scatter(s):
@@ -207,11 +212,16 @@ def tile_list_masking_tone_page_kernel(
 
         def pick(s):
             g, t = divmod(s, PACK)
-            picked = keep.tile([P, M], F32, name="picked%d" % s, tag="low0")
+            picked = keep.tile([P, M], F32, name="picked%d" % s, tag=("low0" if s else "picked0"), align_bytes=64)
             nc.vector.tensor_copy(out=picked[:], in_=pages[s][:].indirect(idx3[:]))
-            nc.scalar.activation(
-                out=x_bf[g][:, :, t], in_=picked[:], func=ACT.Identity, bias=b2_t[:, g, t : t + 1], scale=1.0
-            )
+            if s == SLICES - 1:
+                nc.vector.tensor_scalar(
+                    out=x_bf[g][:, :, t], in0=picked[:], scalar1=b2_t[:, g, t : t + 1], scalar2=None, op0=ALU.add
+                )
+            else:
+                nc.scalar.activation(
+                    out=x_bf[g][:, :, t], in_=picked[:], func=ACT.Identity, bias=b2_t[:, g, t : t + 1], scale=1.0
+                )
             if t == PACK - 1:
                 nc.vector.quantize_mx(
                     out=x_c[g][:].bitcast(FP8X4), scales=x_s[g][:], in_=x_bf[g][:].rearrange("p m t -> p (m t)")
@@ -241,7 +251,7 @@ def tile_list_masking_tone_page_kernel(
         def quantize_page(g, c):
             if c == 0:
                 planes[g] = (
-                    keep.tile([P, T2], U32, name="page_c%d" % g, tag="h%d" % g, align_bytes=64),
+                    keep.tile([P, T2], U32, name="page_c%d" % g, tag=("wg_first", "page_c")[g], align_bytes=64),
                     keep.tile([P, T2], U8, name="page_s%d" % g, align_bytes=64),
                 )
             codes, scales = planes[g]
@@ -270,37 +280,55 @@ def tile_list_masking_tone_page_kernel(
         def finish(n):
             size = keep.tile([P, M], F32, name="size%d" % n, tag="size", bufs=2)
             nc.scalar.activation(out=size[:], in_=tones[n][:], func=ACT.Abs)
-            cosine = keep.tile([P, M], F32, name="cosine%d" % n, tag="cosine", bufs=2)
+            cosine = keep.tile([P, M], F32, name="cosine%d" % n, tag="cosine", bufs=3)
             nc.scalar.activation(out=cosine[:], in_=size[:], func=ACT.Sin, scale=-1.0, bias=math.pi / 2)
-            y = keep.tile([P, M], F32, name="y%d" % n, tag="y", bufs=3)
+            y = keep.tile([P, M], F32, name="y%d" % n, tag="y", bufs=TILES)
             nc.vector.tensor_tensor(out=y[:], in0=tones[n][:], in1=cosine[:], op=ALU.mult)
             nc.sync.dma_start(out=out_0[n * P : (n + 1) * P, :], in_=y[:])
 
+        probe = keep.tile([P, 2], F32, name="probe")
         make_h(0)
+        load_page(4)
+        load_w2(0)
         for s in range(SLICES):
             scatter(s)
             if s + 1 < SLICES:
                 make_h(s + 1)
             pick(s)
-            if s == 1:
+            if s == 0:
+                load_page(5)
+                load_w2(1)
+                load_page(6)
                 quantize_w1(1)
-            if s in (2, 3):
-                quantize_w2(s - 2)
+                load_page(7)
+            if s == 0:
+                round_page(0)
+            if s == 1:
+                round_page(1)
+            if s == 2:
+                round_page(2)
+                quantize_w2(0, 0)
+            if s == 3:
+                round_page(3)
+                quantize_w2(0, 1)
+            if s == 4:
+                weave(0, 0, nc.scalar.copy)
+                weave(0, 1, nc.scalar.copy)
+                weave(0, 2, nc.scalar.copy)
+                weave(0, 3, nc.scalar.copy)
             if s == 5:
-                for n in range(4):
-                    tone_pass(0, n)
+                round_page(4)
+                quantize_w2(1, 0)
+                [tone_pass(0, n) for n in range(4)]
             if s == 6:
-                for n in range(4, TILES):
-                    tone_pass(0, n)
-                for c in range(CHUNKS):
-                    quantize_page(0, c)
-            if 1 <= s < SLICES - 1:
-                round_page(s - 1)
-            if s == PACK:
-                for c in range(CHUNKS):
-                    weave(0, c, nc.scalar.copy)
-            if s == SLICES - 2:
-                round_page(s)
+                [tone_pass(0, n) for n in range(4, TILES)]
+                round_page(5)
+                quantize_w2(1, 1)
+                round_page(6)
+                quantize_page(0, 0)
+                quantize_page(0, 1)
+                quantize_page(0, 2)
+                quantize_page(0, 3)
         for n in range(TILES):
             tone_pass(1, n)
         round_page(SLICES - 1)

@@ -23,12 +23,18 @@ PASS = P * PACK
 GROUPS = H // PASS
 SLICES = GROUPS * PACK
 BANK = 512
+BANKS = 8
 HALVES = S // BANK
-QUADS = 4
+QUAD = 32
+SCALE_ROWS = 4
+QUAD_ORDER = (0, 2, 1, 3)
+PER_COLUMN = 16
 CHUNK = 512
 CHUNKS = T2 // CHUNK
 TILES = N // P
-PAGE_SLOTS = ("page0", "page1", "page2", "page3", "low00", "low10", "picked0", "w1_raw")
+LINE = 4
+W2_PARTS = ((0, 512), (512, N))
+PAGE_TAGS = ("warm_out", "w1_bf0", "tab_s", "tab_w", "low00", "low10", "picked0", "w1_raw")
 
 
 def tile_list_masking_tone_page_kernel(
@@ -41,64 +47,73 @@ def tile_list_masking_tone_page_kernel(
         keep = ctx.enter_context(tc.tile_pool(name="keep", bufs=1))
         psum = ctx.enter_context(tc.psum_pool(name="psum", bufs=1))
 
-        idx = lists.tile([P, S // 16], U16, name="idx")
-        idx2 = lists.tile([P, S // 16], U16, name="idx2")
-        idx3 = lists.tile([P, M // 16], U16, name="idx3")
+        def sbuf(shape, dtype, name, tag=None, bufs=1):
+            return keep.tile(shape, dtype, name=name, tag=tag or name, bufs=bufs, align_bytes=64)
 
-        tab_s = keep.tile([P, T], U8, name="tab_s", tag="page2", align_bytes=64)
-        w4_s_raw = keep.tile([P, H], U8, name="w4_s_raw", tag="wg_first", align_bytes=64)
-        nc.vector.memset(tab_s[:].bitcast(I32), 0)
+        def quad(q, rows=QUAD):
+            return slice(QUAD * q, QUAD * q + rows)
 
-        warm_in = keep.tile([P, 1], F32, name="warm_in", tag="page3", align_bytes=64)
-        warm_out = keep.tile([P, 1], F32, name="warm_out", tag="page0", align_bytes=64)
-        nc.gpsimd.memset(warm_in[:], 0.0)
-        nc.scalar.activation(out=warm_out[:], in_=warm_in[:], func=ACT.Sin)
+        def scale_rows(q):
+            return slice(SCALE_ROWS * q, SCALE_ROWS * (q + 1))
+
         w1_rows = w1.rearrange("(p j) (g c) -> g p j c", j=PACK, c=PASS)
         w2_rows = w2.rearrange("(g p j) n -> g p j n", p=P, j=PACK)
         page_rows = page0.rearrange("(g p t) c -> g t p c", p=P, t=PACK)
         out_rows = out_1.rearrange("(g p t) c -> g t p c", p=P, t=PACK)
-        wgs_rows = wgs.rearrange("(q t) j -> q t j", t=PACK)
+        wgs_rows = wgs.rearrange("(a t) j -> a t j", t=PACK)
 
-        thr_t = keep.tile([P, GROUPS, PACK], F32, name="thr_t", tag="thr_t")
-        w4_raw = keep.tile([P, 2 * H], U8, name="w4_raw", tag="wg_rest", align_bytes=64)
-        tab_w = keep.tile([P, T], U32, name="tab_w", tag="page3", align_bytes=64)
-        w1_raw = {0: keep.tile([P, PACK, PASS], F32, name="w1_raw0", tag="w1_raw", align_bytes=64)}
+        tab_s = sbuf([P, T], U8, "tab_s")
+        nc.vector.memset(tab_s[:].bitcast(I32), 0)
 
+        warm_in = sbuf([P, 1], F32, "warm_in", tag="tab_w")
+        warm_out = sbuf([P, 1], F32, "warm_out")
+        nc.gpsimd.memset(warm_in[:], 0.0)
+        nc.scalar.activation(out=warm_out[:], in_=warm_in[:], func=ACT.Sin)
+
+        idx = lists.tile([P, S // PER_COLUMN], U16, name="idx")
+        idx2 = lists.tile([P, S // PER_COLUMN], U16, name="idx2")
+        idx3 = lists.tile([P, M // PER_COLUMN], U16, name="idx3")
         nc.sync.dma_start(out=idx[:], in_=offs)
         nc.sync.dma_start(out=idx2[:], in_=offs2)
         nc.sync.dma_start(out=idx3[:], in_=offs3)
-        for q in range(QUADS):
+        w4_s_raw = sbuf([P, H], U8, "w4_s_raw")
+        for q in QUAD_ORDER:
+            rows = w4_scales[0, scale_rows(q), :].bitcast(I32)
             nc.sync.dma_start(
-                out=w4_s_raw[32 * q : 32 * q + 32, :].bitcast(I32),
-                in_=w4_scales[0, 4 * q : 4 * q + 4, :].bitcast(I32).unsqueeze(0).broadcast_to([8, 4, H // 4]),
+                out=w4_s_raw[quad(q), :].bitcast(I32),
+                in_=rows.unsqueeze(0).broadcast_to([QUAD // SCALE_ROWS, SCALE_ROWS, H // 4]),
             )
-        nc.sync.dma_start(out=w1_raw[0][:], in_=w1_rows[0])
+        w1_raw = {}
+
+        def load_w1(g):
+            w1_raw[g] = sbuf([P, PACK, PASS], F32, "w1_raw%d" % g, tag="w1_raw")
+            nc.sync.dma_start(out=w1_raw[g][:], in_=w1_rows[g])
+
+        load_w1(0)
+        w4_raw = sbuf([P, 2 * H], U8, "w4_raw")
         nc.sync.dma_start(out=w4_raw[:].bitcast(I32), in_=w4_words[0].bitcast(I32))
+        thr_t = sbuf([P, GROUPS, PACK], F32, "thr_t")
         nc.sync.dma_start(out=thr_t[:], in_=thr.rearrange("(g p t) -> p g t", p=P, t=PACK))
-        for q in range(QUADS):
+        for q in QUAD_ORDER:
             nc.sync.dma_start(
-                out=tab_s[32 * q : 32 * q + 4, :].bitcast(I32),
-                in_=tab_scales[0, 4 * q : 4 * q + 4, :].bitcast(I32),
+                out=tab_s[quad(q, SCALE_ROWS), :].bitcast(I32), in_=tab_scales[0, scale_rows(q), :].bitcast(I32)
             )
-        nc.sync.dma_start(
-            out=tab_w[:].bitcast(I32), in_=tab_words[0].rearrange("p c i -> p (c i)").bitcast(I32)
-        )
+        tab_w = sbuf([P, T], U32, "tab_w")
+        nc.sync.dma_start(out=tab_w[:].bitcast(I32), in_=tab_words[0].rearrange("p c i -> p (c i)").bitcast(I32))
 
         pages = {}
 
         def load_page(s):
-            pages[s] = keep.tile([P, T2], F32, name="page%d" % s, tag=PAGE_SLOTS[s], align_bytes=64)
+            pages[s] = sbuf([P, T2], F32, "page%d" % s, tag=PAGE_TAGS[s])
             nc.sync.dma_start(out=pages[s][:], in_=page_rows[s // PACK, s % PACK])
 
         load_page(0)
 
-        neg_thr = keep.tile([P, GROUPS, PACK], F32, name="neg_thr")
-        nc.gpsimd.tensor_scalar(
-            out=neg_thr[:], in0=thr_t[:], scalar1=-1.0, scalar2=0.0, op0=ALU.mult, op1=ALU.add
-        )
+        neg_thr = sbuf([P, GROUPS, PACK], F32, "neg_thr")
+        nc.gpsimd.tensor_scalar(out=neg_thr[:], in0=thr_t[:], scalar1=-1.0, scalar2=0.0, op0=ALU.mult, op1=ALU.add)
 
-        w4_c = keep.tile([P, 2 * H], U8, name="w4_c", align_bytes=64)
-        w4_s = keep.tile([P, H], U8, name="w4_s", align_bytes=64)
+        w4_c = sbuf([P, 2 * H], U8, "w4_c")
+        w4_s = sbuf([P, H], U8, "w4_s")
         nc.vector.tensor_copy(
             out=w4_c[:].rearrange("p (g t m e) -> p g m t e", g=GROUPS, t=PACK, e=2),
             in_=w4_raw[:].rearrange("p (g m t e) -> p g m t e", g=GROUPS, t=PACK, e=2),
@@ -108,120 +123,104 @@ def tile_list_masking_tone_page_kernel(
             in_=w4_s_raw[:].rearrange("p (g m t) -> p g m t", g=GROUPS, t=PACK),
         )
 
-        wg_first = keep.tile([P, S], F32, name="wg_first", tag="wg_first", align_bytes=64)
-        for q in range(QUADS):
-            nc.sync.dma_start(out=wg_first[32 * q : 32 * q + 32, :], in_=wgs_rows[:, 0, :])
+        wg_first = sbuf([P, S], F32, "wg_first", tag="w4_s_raw")
+        for q in QUAD_ORDER:
+            nc.sync.dma_start(out=wg_first[quad(q), :], in_=wgs_rows[:, 0, :])
 
-        w1_c = [keep.tile([P, PASS], U32, name="w1_c%d" % g, align_bytes=64) for g in range(GROUPS)]
-        w1_s = [keep.tile([P, PASS], U8, name="w1_s%d" % g, align_bytes=64) for g in range(GROUPS)]
+        w1_c = [sbuf([P, PASS], U32, "w1_c%d" % g) for g in range(GROUPS)]
+        w1_s = [sbuf([P, PASS], U8, "w1_s%d" % g) for g in range(GROUPS)]
 
         def quantize_w1(g):
-            grouped = keep.tile([P, PACK * PASS], BF16, name="w1_bf%d" % g, tag=("page1", "w1_bf1")[g], align_bytes=64)
+            grouped = sbuf([P, PACK * PASS], BF16, "w1_bf%d" % g)
             nc.scalar.copy(
                 out=grouped[:].rearrange("p (t m j) -> p m j t", t=PACK, j=PACK),
                 in_=w1_raw[g][:].rearrange("p j (m t) -> p m j t", t=PACK),
             )
             nc.vector.quantize_mx(out=w1_c[g][:].bitcast(FP8X4), scales=w1_s[g][:], in_=grouped[:])
 
-        v_s = keep.tile([P, S], U8, name="v_s", align_bytes=64)
+        v_s = sbuf([P, S], U8, "v_s")
         nc.vector.tensor_copy(out=v_s[:], in_=tab_s[:].indirect(idx[:]))
         quantize_w1(0)
-        v_c = [
-            keep.tile([P, BANK], U32, name="v_c0", align_bytes=64),
-            keep.tile([P, BANK], U32, name="v_c1", align_bytes=64),
-        ]
+        v_c = [sbuf([P, BANK], U32, "v_c%d" % u) for u in range(HALVES)]
         for u in range(HALVES):
-            cols = BANK // 16
-            nc.vector.tensor_copy(out=v_c[u][:], in_=tab_w[:].indirect(idx[:, u * cols : (u + 1) * cols]))
+            part = slice(u * BANK // PER_COLUMN, (u + 1) * BANK // PER_COLUMN)
+            nc.vector.tensor_copy(out=v_c[u][:], in_=tab_w[:].indirect(idx[:, part]))
 
-        wg_rest = keep.tile([P, PACK - 1, S], F32, name="wg_rest", tag="wg_rest", align_bytes=64)
-        for q in range(QUADS):
-            nc.sync.dma_start(out=wg_rest[32 * q : 32 * q + 32, :, :], in_=wgs_rows[:, 1:PACK, :])
+        wg_rest = sbuf([P, PACK - 1, S], F32, "wg_rest", tag="w4_raw")
+        for q in QUAD_ORDER:
+            nc.sync.dma_start(out=wg_rest[quad(q), 0, :], in_=wgs_rows[:, 1, :])
         load_page(1)
-        b2_t = keep.tile([P, GROUPS, PACK], F32, name="b2_t", tag="thr_t")
+        for q in QUAD_ORDER:
+            nc.sync.dma_start(out=wg_rest[quad(q), 1:, :], in_=wgs_rows[:, 2:, :])
+        b2_t = sbuf([P, GROUPS, PACK], F32, "b2_t", tag="thr_t")
         nc.sync.dma_start(out=b2_t[:], in_=b2.rearrange("(g p t) -> p g t", p=P, t=PACK))
-        w1_raw[1] = keep.tile([P, PACK, PASS], F32, name="w1_raw1", tag="w1_raw", align_bytes=64)
-        nc.sync.dma_start(out=w1_raw[1][:], in_=w1_rows[1])
+        load_w1(1)
         load_page(2)
         load_page(3)
 
-        w2_c = [keep.tile([P, N], U32, name="w2_c%d" % g, align_bytes=64) for g in range(GROUPS)]
-        w2_s = [keep.tile([P, N], U8, name="w2_s%d" % g, align_bytes=64) for g in range(GROUPS)]
-
         w2_raw = {}
+        w2_c = [sbuf([P, N], U32, "w2_c%d" % g) for g in range(GROUPS)]
+        w2_s = [sbuf([P, N], U8, "w2_s%d" % g) for g in range(GROUPS)]
 
         def load_w2(g):
-            w2_raw[g] = keep.tile([P, PACK, N], F32, name="w2_raw%d" % g, tag="low%d1" % g, align_bytes=64)
+            w2_raw[g] = sbuf([P, PACK, N], F32, "w2_raw%d" % g, tag="low%d1" % g)
             nc.sync.dma_start(out=w2_raw[g][:], in_=w2_rows[g])
 
         def quantize_w2(g, part):
-            raw = w2_raw[g]
-            for lo, hi in (((0, 512), (512, N))[part],):
-                grouped = keep.tile([P, PACK * (hi - lo)], BF16, name="w2_bf%d_%d" % (g, part), tag="w2_bf%d" % part, align_bytes=64)
-                nc.scalar.copy(
-                    out=grouped[:].rearrange("p (c i j) -> p c j i", i=4, j=PACK),
-                    in_=raw[:, :, lo:hi].rearrange("p j (c i) -> p c j i", i=4),
-                )
-                nc.vector.quantize_mx(
-                    out=w2_c[g][:, lo:hi].bitcast(FP8X4),
-                    scales=w2_s[g][:, lo:hi],
-                    in_=grouped[:],
-                )
+            lo, hi = W2_PARTS[part]
+            grouped = sbuf([P, PACK * (hi - lo)], BF16, "w2_bf%d_%d" % (g, part), tag="w2_bf%d" % part)
+            nc.scalar.copy(
+                out=grouped[:].rearrange("p (a i j) -> p a j i", i=LINE, j=PACK),
+                in_=w2_raw[g][:, :, lo:hi].rearrange("p j (a i) -> p a j i", i=LINE),
+            )
+            nc.vector.quantize_mx(out=w2_c[g][:, lo:hi].bitcast(FP8X4), scales=w2_s[g][:, lo:hi], in_=grouped[:])
 
-        h_tiles = {}
-        x_bf = [keep.tile([P, M, PACK], BF16, name="x_bf%d" % g, align_bytes=64) for g in range(GROUPS)]
-        x_c = [keep.tile([P, M], U32, name="x_c%d" % g, align_bytes=64) for g in range(GROUPS)]
-        x_s = [keep.tile([P, M], U8, name="x_s%d" % g, align_bytes=64) for g in range(GROUPS)]
+        h = {}
 
         def make_h(s):
             g, t = divmod(s, PACK)
-            cols = slice(t * P, (t + 1) * P)
-            c4 = g * PASS + t * P
-            h = keep.tile([P, S], F32, name="h%d" % s, tag="h")
-            h_tiles[s] = h
+            w1_cols = slice(t * P, (t + 1) * P)
+            first = g * PASS + t * P
+            shift = neg_thr[:, g, t : t + 1]
+            h[s] = sbuf([P, S], F32, "h%d" % s, tag="h")
             for u in range(HALVES):
                 half = slice(u * BANK, (u + 1) * BANK)
                 left = psum.tile([P, BANK], F32, name="left%d_%d" % (s, u), tag="bank%d" % u)
                 nc.tensor.matmul_mx(
-                    out=left[:], lhsT=w1_c[g][:, cols].bitcast(FP8X4), lhsT_scale=w1_s[g][:, cols],
+                    out=left[:], lhsT=w1_c[g][:, w1_cols].bitcast(FP8X4), lhsT_scale=w1_s[g][:, w1_cols],
                     rhs=v_c[u][:].bitcast(FP8X4), rhs_scale=v_s[:, half], start=True, stop=True,
                 )
-                low = keep.tile(
-                    [P, BANK], F32, name="low%d_%d" % (s, u),
-                    tag=("low%d" % u if s > 1 else "low%d%d" % (s, u)), align_bytes=64,
-                )
-                nc.scalar.activation(
-                    out=low[:], in_=left[:], func=ACT.Identity, bias=neg_thr[:, g, t : t + 1], scale=1.0
-                )
+                low = sbuf([P, BANK], F32, "low%d%d" % (s, u), tag="low%d" % u if s > 1 else None)
+                nc.scalar.activation(out=low[:], in_=left[:], func=ACT.Identity, bias=shift, scale=1.0)
                 right = psum.tile([P, BANK], F32, name="right%d_%d" % (s, u), tag="bank%d" % (HALVES + u))
                 nc.tensor.matmul_mx(
-                    out=right[:], lhsT=w4_c[:, 2 * c4 : 2 * (c4 + P)].bitcast(FP4X4),
-                    lhsT_scale=w4_s[:, c4 : c4 + P],
+                    out=right[:], lhsT=w4_c[:, 2 * first : 2 * (first + P)].bitcast(FP4X4),
+                    lhsT_scale=w4_s[:, first : first + P],
                     rhs=v_c[u][:].bitcast(FP8X4), rhs_scale=v_s[:, half], start=True, stop=True,
                 )
                 nc.vector.scalar_tensor_tensor(
-                    out=h[:, half], in0=right[:], scalar=neg_thr[:, g, t : t + 1],
-                    in1=low[:], op0=ALU.add, op1=ALU.min,
+                    out=h[s][:, half], in0=right[:], scalar=shift, in1=low[:], op0=ALU.add, op1=ALU.min
                 )
 
         def scatter(s):
             g, t = divmod(s, PACK)
             wg = wg_first[:] if t == 0 else wg_rest[:, t - 1, :]
-            nc.vector.tensor_tensor(out=pages[s][:].indirect(idx2[:]), in0=h_tiles[s][:], in1=wg, op=ALU.mult)
+            nc.vector.tensor_tensor(out=pages[s][:].indirect(idx2[:]), in0=h[s][:], in1=wg, op=ALU.mult)
             nc.sync.dma_start(out=out_rows[g, t], in_=pages[s][:])
+
+        x_bf = [sbuf([P, M, PACK], BF16, "x_bf%d" % g) for g in range(GROUPS)]
+        x_c = [sbuf([P, M], U32, "x_c%d" % g) for g in range(GROUPS)]
+        x_s = [sbuf([P, M], U8, "x_s%d" % g) for g in range(GROUPS)]
 
         def pick(s):
             g, t = divmod(s, PACK)
-            picked = keep.tile([P, M], F32, name="picked%d" % s, tag=("low0" if s else "picked0"), align_bytes=64)
+            bias = b2_t[:, g, t : t + 1]
+            picked = sbuf([P, M], F32, "picked%d" % s, tag="low0" if s else None)
             nc.vector.tensor_copy(out=picked[:], in_=pages[s][:].indirect(idx3[:]))
             if s == SLICES - 1:
-                nc.vector.tensor_scalar(
-                    out=x_bf[g][:, :, t], in0=picked[:], scalar1=b2_t[:, g, t : t + 1], scalar2=None, op0=ALU.add
-                )
+                nc.vector.tensor_scalar(out=x_bf[g][:, :, t], in0=picked[:], scalar1=bias, scalar2=None, op0=ALU.add)
             else:
-                nc.scalar.activation(
-                    out=x_bf[g][:, :, t], in_=picked[:], func=ACT.Identity, bias=b2_t[:, g, t : t + 1], scale=1.0
-                )
+                nc.scalar.activation(out=x_bf[g][:, :, t], in_=picked[:], func=ACT.Identity, bias=bias, scale=1.0)
             if t == PACK - 1:
                 nc.vector.quantize_mx(
                     out=x_c[g][:].bitcast(FP8X4), scales=x_s[g][:], in_=x_bf[g][:].rearrange("p m t -> p (m t)")
@@ -229,30 +228,28 @@ def tile_list_masking_tone_page_kernel(
 
         pairs = {}
         woven = {}
+        planes = {}
 
         def round_page(s):
             g, t = divmod(s, PACK)
             for c in range(CHUNKS):
                 if t == 0:
-                    pairs[g, c] = keep.tile([P, 2, CHUNK, 2], BF16, name="pairs%d_%d" % (g, c), tag="pairs%d" % c)
+                    pairs[g, c] = sbuf([P, 2, CHUNK, 2], BF16, "pairs%d_%d" % (g, c), tag="pairs%d" % c)
                 nc.scalar.copy(out=pairs[g, c][:, t // 2, :, t % 2], in_=pages[s][:, c * CHUNK : (c + 1) * CHUNK])
 
         def weave(g, c, copy):
-            tile = keep.tile([P, CHUNK * PACK], BF16, name="woven%d_%d" % (g, c), tag="woven%d" % c, align_bytes=64)
-            woven[g, c] = tile
-            words = pairs[g, c][:].rearrange("p u m e -> p (u m e)").bitcast(F32)
+            woven[g, c] = sbuf([P, CHUNK * PACK], BF16, "woven%d_%d" % (g, c), tag="woven%d" % c)
+            rows = pairs[g, c][:].rearrange("p u m e -> p (u m e)").bitcast(F32)
             copy(
-                out=tile[:].bitcast(F32).rearrange("p (a i u) -> p a u i", i=4, u=2),
-                in_=words.rearrange("p (u a i) -> p a u i", i=4, u=2),
+                out=woven[g, c][:].bitcast(F32).rearrange("p (a i u) -> p a u i", i=LINE, u=2),
+                in_=rows.rearrange("p (u a i) -> p a u i", i=LINE, u=2),
             )
-
-        planes = {}
 
         def quantize_page(g, c):
             if c == 0:
                 planes[g] = (
-                    keep.tile([P, T2], U32, name="page_c%d" % g, tag=("wg_first", "page_c")[g], align_bytes=64),
-                    keep.tile([P, T2], U8, name="page_s%d" % g, align_bytes=64),
+                    sbuf([P, T2], U32, "page_c%d" % g, tag="w4_s_raw" if g == 0 else None),
+                    sbuf([P, T2], U8, "page_s%d" % g),
                 )
             codes, scales = planes[g]
             words = out_2[g].rearrange("p c i -> p (c i)").bitcast(I32)
@@ -260,17 +257,17 @@ def tile_list_masking_tone_page_kernel(
             nc.vector.quantize_mx(out=codes[:, cols].bitcast(FP8X4), scales=scales[:, cols], in_=woven[g, c][:])
             nc.sync.dma_start(out=words[:, cols], in_=codes[:, cols].bitcast(I32))
             if c == CHUNKS - 1:
-                for q in range(QUADS):
+                for q in QUAD_ORDER:
                     nc.sync.dma_start(
-                        out=out_3[g, 4 * q : 4 * q + 4, :].bitcast(I32),
-                        in_=scales[32 * q : 32 * q + 4, :].bitcast(I32),
+                        out=out_3[g, scale_rows(q), :].bitcast(I32), in_=scales[quad(q, SCALE_ROWS), :].bitcast(I32)
                     )
 
         tones = {}
+        spare_banks = BANKS - 2 * HALVES
 
         def tone_pass(g, n):
             if g == 0:
-                tones[n] = psum.tile([P, M], F32, name="tone%d" % n, tag="bank%d" % ((2 * HALVES + n) % 8))
+                tones[n] = psum.tile([P, M], F32, name="tone%d" % n, tag="bank%d" % ((2 * HALVES + n) % BANKS))
             cols = slice(n * P, (n + 1) * P)
             nc.tensor.matmul_mx(
                 out=tones[n][:], lhsT=w2_c[g][:, cols].bitcast(FP8X4), lhsT_scale=w2_s[g][:, cols],
@@ -278,57 +275,56 @@ def tile_list_masking_tone_page_kernel(
             )
 
         def finish(n):
-            size = keep.tile([P, M], F32, name="size%d" % n, tag="size", bufs=2)
+            size = sbuf([P, M], F32, "size%d" % n, tag="size", bufs=2)
             nc.scalar.activation(out=size[:], in_=tones[n][:], func=ACT.Abs)
-            cosine = keep.tile([P, M], F32, name="cosine%d" % n, tag="cosine", bufs=3)
+            cosine = sbuf([P, M], F32, "cosine%d" % n, tag="cosine", bufs=3)
             nc.scalar.activation(out=cosine[:], in_=size[:], func=ACT.Sin, scale=-1.0, bias=math.pi / 2)
-            y = keep.tile([P, M], F32, name="y%d" % n, tag="y", bufs=TILES)
+            y = sbuf([P, M], F32, "y%d" % n)
             nc.vector.tensor_tensor(out=y[:], in0=tones[n][:], in1=cosine[:], op=ALU.mult)
             nc.sync.dma_start(out=out_0[n * P : (n + 1) * P, :], in_=y[:])
 
-        probe = keep.tile([P, 2], F32, name="probe")
-        make_h(0)
-        load_page(4)
-        load_w2(0)
-        for s in range(SLICES):
+        def step(s):
             scatter(s)
             if s + 1 < SLICES:
                 make_h(s + 1)
             pick(s)
-            if s == 0:
-                load_page(5)
-                load_w2(1)
-                load_page(6)
-                quantize_w1(1)
-                load_page(7)
-            if s == 0:
-                round_page(0)
-            if s == 1:
-                round_page(1)
-            if s == 2:
-                round_page(2)
-                quantize_w2(0, 0)
-            if s == 3:
-                round_page(3)
-                quantize_w2(0, 1)
-            if s == 4:
-                weave(0, 0, nc.scalar.copy)
-                weave(0, 1, nc.scalar.copy)
-                weave(0, 2, nc.scalar.copy)
-                weave(0, 3, nc.scalar.copy)
-            if s == 5:
-                round_page(4)
-                quantize_w2(1, 0)
-                [tone_pass(0, n) for n in range(4)]
-            if s == 6:
-                [tone_pass(0, n) for n in range(4, TILES)]
-                round_page(5)
-                quantize_w2(1, 1)
-                round_page(6)
-                quantize_page(0, 0)
-                quantize_page(0, 1)
-                quantize_page(0, 2)
-                quantize_page(0, 3)
+
+        make_h(0)
+        load_page(4)
+        load_w2(0)
+        step(0)
+        load_page(5)
+        load_w2(1)
+        load_page(6)
+        quantize_w1(1)
+        load_page(7)
+        round_page(0)
+        step(1)
+        round_page(1)
+        step(2)
+        round_page(2)
+        quantize_w2(0, 0)
+        step(3)
+        round_page(3)
+        quantize_w2(0, 1)
+        step(4)
+        for c in range(CHUNKS):
+            weave(0, c, nc.scalar.copy)
+        step(5)
+        round_page(4)
+        quantize_w2(1, 0)
+        for n in range(spare_banks):
+            tone_pass(0, n)
+        step(6)
+        for n in range(spare_banks, TILES):
+            tone_pass(0, n)
+        round_page(5)
+        quantize_w2(1, 1)
+        round_page(6)
+        for c in range(CHUNKS):
+            quantize_page(0, c)
+        step(7)
+
         for n in range(TILES):
             tone_pass(1, n)
         round_page(SLICES - 1)

@@ -27,14 +27,15 @@ BANKS = 8
 HALVES = S // BANK
 QUAD = 32
 SCALE_ROWS = 4
-QUAD_ORDER = (0, 2, 1, 3)
+QUADS = P // QUAD
 PER_COLUMN = 16
 CHUNK = 512
 CHUNKS = T2 // CHUNK
 TILES = N // P
 LINE = 4
 W2_PARTS = ((0, 512), (512, N))
-PAGE_TAGS = ("warm_out", "w1_bf0", "tab_s", "tab_w", "low00", "low10", "picked0", "w1_raw")
+OWN_LOW = ((0, 0), (0, 1), (1, 0), (1, 1), (2, 1), (3, 1))
+PAGE_TAGS = ("warm_out", "tab_s", "tab_w", "low00", "low01", "low10", "picked0", "w1_raw")
 
 
 def tile_list_masking_tone_page_kernel(
@@ -77,7 +78,7 @@ def tile_list_masking_tone_page_kernel(
         nc.sync.dma_start(out=idx2[:], in_=offs2)
         nc.sync.dma_start(out=idx3[:], in_=offs3)
         w4_s_raw = sbuf([P, H], U8, "w4_s_raw")
-        for q in QUAD_ORDER:
+        for q in range(QUADS):
             rows = w4_scales[0, scale_rows(q), :].bitcast(I32)
             nc.sync.dma_start(
                 out=w4_s_raw[quad(q), :].bitcast(I32),
@@ -94,7 +95,7 @@ def tile_list_masking_tone_page_kernel(
         nc.sync.dma_start(out=w4_raw[:].bitcast(I32), in_=w4_words[0].bitcast(I32))
         thr_t = sbuf([P, GROUPS, PACK], F32, "thr_t")
         nc.sync.dma_start(out=thr_t[:], in_=thr.rearrange("(g p t) -> p g t", p=P, t=PACK))
-        for q in QUAD_ORDER:
+        for q in range(QUADS):
             nc.sync.dma_start(
                 out=tab_s[quad(q, SCALE_ROWS), :].bitcast(I32), in_=tab_scales[0, scale_rows(q), :].bitcast(I32)
             )
@@ -124,46 +125,52 @@ def tile_list_masking_tone_page_kernel(
         )
 
         wg_first = sbuf([P, S], F32, "wg_first", tag="w4_s_raw")
-        for q in QUAD_ORDER:
+        for q in range(QUADS):
             nc.sync.dma_start(out=wg_first[quad(q), :], in_=wgs_rows[:, 0, :])
 
-        w1_c = [sbuf([P, PASS], U32, "w1_c%d" % g) for g in range(GROUPS)]
+        w1_bf = {}
+        w1_c = {}
         w1_s = [sbuf([P, PASS], U8, "w1_s%d" % g) for g in range(GROUPS)]
 
-        def quantize_w1(g):
-            grouped = sbuf([P, PACK * PASS], BF16, "w1_bf%d" % g)
+        def round_w1(g):
+            w1_bf[g] = sbuf([P, PACK * PASS], BF16, "w1_bf%d" % g)
             nc.scalar.copy(
-                out=grouped[:].rearrange("p (t m j) -> p m j t", t=PACK, j=PACK),
+                out=w1_bf[g][:].rearrange("p (t m j) -> p m j t", t=PACK, j=PACK),
                 in_=w1_raw[g][:].rearrange("p j (m t) -> p m j t", t=PACK),
             )
-            nc.vector.quantize_mx(out=w1_c[g][:].bitcast(FP8X4), scales=w1_s[g][:], in_=grouped[:])
+
+        def quantize_w1(g):
+            w1_c[g] = sbuf([P, PASS], U32, "w1_c%d" % g, tag="low31" if g else None)
+            nc.vector.quantize_mx(out=w1_c[g][:].bitcast(FP8X4), scales=w1_s[g][:], in_=w1_bf[g][:])
 
         v_s = sbuf([P, S], U8, "v_s")
         nc.vector.tensor_copy(out=v_s[:], in_=tab_s[:].indirect(idx[:]))
+        round_w1(0)
         quantize_w1(0)
         v_c = [sbuf([P, BANK], U32, "v_c%d" % u) for u in range(HALVES)]
         for u in range(HALVES):
             part = slice(u * BANK // PER_COLUMN, (u + 1) * BANK // PER_COLUMN)
             nc.vector.tensor_copy(out=v_c[u][:], in_=tab_w[:].indirect(idx[:, part]))
 
-        wg_rest = sbuf([P, PACK - 1, S], F32, "wg_rest", tag="w4_raw")
-        for q in QUAD_ORDER:
-            nc.sync.dma_start(out=wg_rest[quad(q), 0, :], in_=wgs_rows[:, 1, :])
+        wg_second = sbuf([P, S], F32, "wg_second", tag="w4_raw")
+        for q in range(QUADS):
+            nc.sync.dma_start(out=wg_second[quad(q), :], in_=wgs_rows[:, 1, :])
         load_page(1)
-        for q in QUAD_ORDER:
-            nc.sync.dma_start(out=wg_rest[quad(q), 1:, :], in_=wgs_rows[:, 2:, :])
+        wg_rest = sbuf([P, 2, S], F32, "wg_rest", tag="w1_bf0")
+        for q in range(QUADS):
+            nc.sync.dma_start(out=wg_rest[quad(q), :, :], in_=wgs_rows[:, 2:, :])
+        wg = (wg_first[:], wg_second[:], wg_rest[:, 0, :], wg_rest[:, 1, :])
         b2_t = sbuf([P, GROUPS, PACK], F32, "b2_t", tag="thr_t")
         nc.sync.dma_start(out=b2_t[:], in_=b2.rearrange("(g p t) -> p g t", p=P, t=PACK))
         load_w1(1)
         load_page(2)
-        load_page(3)
 
         w2_raw = {}
         w2_c = [sbuf([P, N], U32, "w2_c%d" % g) for g in range(GROUPS)]
         w2_s = [sbuf([P, N], U8, "w2_s%d" % g) for g in range(GROUPS)]
 
         def load_w2(g):
-            w2_raw[g] = sbuf([P, PACK, N], F32, "w2_raw%d" % g, tag="low%d1" % g)
+            w2_raw[g] = sbuf([P, PACK, N], F32, "w2_raw%d" % g, tag="low%d1" % (g + 1))
             nc.sync.dma_start(out=w2_raw[g][:], in_=w2_rows[g])
 
         def quantize_w2(g, part):
@@ -190,7 +197,7 @@ def tile_list_masking_tone_page_kernel(
                     out=left[:], lhsT=w1_c[g][:, w1_cols].bitcast(FP8X4), lhsT_scale=w1_s[g][:, w1_cols],
                     rhs=v_c[u][:].bitcast(FP8X4), rhs_scale=v_s[:, half], start=True, stop=True,
                 )
-                low = sbuf([P, BANK], F32, "low%d%d" % (s, u), tag="low%d" % u if s > 1 else None)
+                low = sbuf([P, BANK], F32, "low%d%d" % (s, u), tag=None if (s, u) in OWN_LOW else "low%d" % u)
                 nc.scalar.activation(out=low[:], in_=left[:], func=ACT.Identity, bias=shift, scale=1.0)
                 right = psum.tile([P, BANK], F32, name="right%d_%d" % (s, u), tag="bank%d" % (HALVES + u))
                 nc.tensor.matmul_mx(
@@ -204,8 +211,7 @@ def tile_list_masking_tone_page_kernel(
 
         def scatter(s):
             g, t = divmod(s, PACK)
-            wg = wg_first[:] if t == 0 else wg_rest[:, t - 1, :]
-            nc.vector.tensor_tensor(out=pages[s][:].indirect(idx2[:]), in0=h[s][:], in1=wg, op=ALU.mult)
+            nc.vector.tensor_tensor(out=pages[s][:].indirect(idx2[:]), in0=h[s][:], in1=wg[t], op=ALU.mult)
             nc.sync.dma_start(out=out_rows[g, t], in_=pages[s][:])
 
         x_bf = [sbuf([P, M, PACK], BF16, "x_bf%d" % g) for g in range(GROUPS)]
@@ -257,7 +263,7 @@ def tile_list_masking_tone_page_kernel(
             nc.vector.quantize_mx(out=codes[:, cols].bitcast(FP8X4), scales=scales[:, cols], in_=woven[g, c][:])
             nc.sync.dma_start(out=words[:, cols], in_=codes[:, cols].bitcast(I32))
             if c == CHUNKS - 1:
-                for q in QUAD_ORDER:
+                for q in range(QUADS):
                     nc.sync.dma_start(
                         out=out_3[g, scale_rows(q), :].bitcast(I32), in_=scales[quad(q, SCALE_ROWS), :].bitcast(I32)
                     )
@@ -290,18 +296,20 @@ def tile_list_masking_tone_page_kernel(
             pick(s)
 
         make_h(0)
+        load_page(3)
         load_page(4)
-        load_w2(0)
         step(0)
         load_page(5)
-        load_w2(1)
+        load_w2(0)
         load_page(6)
-        quantize_w1(1)
-        load_page(7)
+        round_w1(1)
         round_page(0)
         step(1)
+        load_w2(1)
+        load_page(7)
         round_page(1)
         step(2)
+        quantize_w1(1)
         round_page(2)
         quantize_w2(0, 0)
         step(3)

import math
from contextlib import ExitStack

import concourse.mybir as mybir

K, T, S, H, T2, M, N = 512, 4096, 1024, 1024, 2048, 512, 768
FLOPS = 2 * (2 * K * H * S + H * N * M)

F32 = mybir.dt.float32
BF16 = mybir.dt.bfloat16
I32 = mybir.dt.int32
U32 = mybir.dt.uint32
U16 = mybir.dt.uint16
U8 = mybir.dt.uint8
FP8X4 = mybir.dt.float8_e4m3fn_x4
FP4X4 = mybir.dt.float4_e2m1fn_x4
ALU = mybir.AluOpType
ACT = mybir.ActivationFunctionType

P = 128
PACK = 4
PASS = P * PACK
GROUPS = H // PASS
SLICES = GROUPS * PACK
BANK = 512
BANKS = 8
HALVES = S // BANK
QUAD = 32
SCALE_ROWS = 4
QUADS = P // QUAD
PER_COLUMN = 16
CHUNK = 512
CHUNKS = T2 // CHUNK
TILES = N // P
LINE = 4
W2_PARTS = ((0, 512), (512, N))
OWN_LOW = ((0, 0), (0, 1), (1, 0), (1, 1), (2, 1), (3, 1))
PAGE_TAGS = ("warm_out", "tab_s", "tab_w", "low00", "low01", "low10", "picked0", "w1_raw")


def tile_list_masking_tone_page_kernel(
    tc, tab_words, tab_scales, offs, w1, w4_words, w4_scales, thr, wgs, page0, offs2, offs3, b2, w2,
    out_0, out_1, out_2, out_3,
):
    nc = tc.nc
    with ExitStack() as ctx:
        lists = ctx.enter_context(tc.tile_pool(name="lists", bufs=1))
        keep = ctx.enter_context(tc.tile_pool(name="keep", bufs=1))
        psum = ctx.enter_context(tc.psum_pool(name="psum", bufs=1))

        def sbuf(shape, dtype, name, tag=None, bufs=1):
            return keep.tile(shape, dtype, name=name, tag=tag or name, bufs=bufs, align_bytes=64)

        def quad(q, rows=QUAD):
            return slice(QUAD * q, QUAD * q + rows)

        def scale_rows(q):
            return slice(SCALE_ROWS * q, SCALE_ROWS * (q + 1))

        w1_rows = w1.rearrange("(p j) (g c) -> g p j c", j=PACK, c=PASS)
        w2_rows = w2.rearrange("(g p j) n -> g p j n", p=P, j=PACK)
        page_rows = page0.rearrange("(g p t) c -> g t p c", p=P, t=PACK)
        out_rows = out_1.rearrange("(g p t) c -> g t p c", p=P, t=PACK)
        wgs_rows = wgs.rearrange("(a t) j -> a t j", t=PACK)

        tab_s = sbuf([P, T], U8, "tab_s")
        nc.vector.memset(tab_s[:].bitcast(I32), 0)

        warm_in = sbuf([P, 1], F32, "warm_in", tag="tab_w")
        warm_out = sbuf([P, 1], F32, "warm_out")
        nc.gpsimd.memset(warm_in[:], 0.0)
        nc.scalar.activation(out=warm_out[:], in_=warm_in[:], func=ACT.Sin)

        idx = lists.tile([P, S // PER_COLUMN], U16, name="idx")
        idx2 = lists.tile([P, S // PER_COLUMN], U16, name="idx2")
        idx3 = lists.tile([P, M // PER_COLUMN], U16, name="idx3")
        nc.sync.dma_start(out=idx[:], in_=offs)
        nc.sync.dma_start(out=idx2[:], in_=offs2)
        nc.sync.dma_start(out=idx3[:], in_=offs3)
        w4_s_raw = sbuf([P, H], U8, "w4_s_raw")
        for q in range(QUADS):
            rows = w4_scales[0, scale_rows(q), :].bitcast(I32)
            nc.sync.dma_start(
                out=w4_s_raw[quad(q), :].bitcast(I32),
                in_=rows.unsqueeze(0).broadcast_to([QUAD // SCALE_ROWS, SCALE_ROWS, H // 4]),
            )
        w1_raw = {}

        def load_w1(g):
            w1_raw[g] = sbuf([P, PACK, PASS], F32, "w1_raw%d" % g, tag="w1_raw")
            nc.sync.dma_start(out=w1_raw[g][:], in_=w1_rows[g])

        load_w1(0)
        w4_raw = sbuf([P, 2 * H], U8, "w4_raw")
        nc.sync.dma_start(out=w4_raw[:].bitcast(I32), in_=w4_words[0].bitcast(I32))
        thr_t = sbuf([P, GROUPS, PACK], F32, "thr_t")
        nc.sync.dma_start(out=thr_t[:], in_=thr.rearrange("(g p t) -> p g t", p=P, t=PACK))
        for q in range(QUADS):
            nc.sync.dma_start(
                out=tab_s[quad(q, SCALE_ROWS), :].bitcast(I32), in_=tab_scales[0, scale_rows(q), :].bitcast(I32)
            )
        tab_w = sbuf([P, T], U32, "tab_w")
        nc.sync.dma_start(out=tab_w[:].bitcast(I32), in_=tab_words[0].rearrange("p c i -> p (c i)").bitcast(I32))

        pages = {}

        def load_page(s):
            pages[s] = sbuf([P, T2], F32, "page%d" % s, tag=PAGE_TAGS[s])
            nc.sync.dma_start(out=pages[s][:], in_=page_rows[s // PACK, s % PACK])

        load_page(0)

        neg_thr = sbuf([P, GROUPS, PACK], F32, "neg_thr")
        nc.gpsimd.tensor_scalar(out=neg_thr[:], in0=thr_t[:], scalar1=-1.0, scalar2=0.0, op0=ALU.mult, op1=ALU.add)

        w4_c = sbuf([P, 2 * H], U8, "w4_c")
        w4_s = sbuf([P, H], U8, "w4_s")
        nc.vector.tensor_copy(
            out=w4_c[:].rearrange("p (g t m e) -> p g m t e", g=GROUPS, t=PACK, e=2),
            in_=w4_raw[:].rearrange("p (g m t e) -> p g m t e", g=GROUPS, t=PACK, e=2),
        )
        nc.vector.tensor_copy(
            out=w4_s[:].rearrange("p (g t m) -> p g m t", g=GROUPS, t=PACK),
            in_=w4_s_raw[:].rearrange("p (g m t) -> p g m t", g=GROUPS, t=PACK),
        )

        wg_first = sbuf([P, S], F32, "wg_first", tag="w4_s_raw")
        for q in range(QUADS):
            nc.sync.dma_start(out=wg_first[quad(q), :], in_=wgs_rows[:, 0, :])

        w1_bf = {}
        w1_c = {}
        w1_s = [sbuf([P, PASS], U8, "w1_s%d" % g) for g in range(GROUPS)]

        def round_w1(g):
            w1_bf[g] = sbuf([P, PACK * PASS], BF16, "w1_bf%d" % g)
            nc.scalar.copy(
                out=w1_bf[g][:].rearrange("p (t m j) -> p m j t", t=PACK, j=PACK),
                in_=w1_raw[g][:].rearrange("p j (m t) -> p m j t", t=PACK),
            )

        def quantize_w1(g):
            w1_c[g] = sbuf([P, PASS], U32, "w1_c%d" % g, tag="low31" if g else None)
            nc.vector.quantize_mx(out=w1_c[g][:].bitcast(FP8X4), scales=w1_s[g][:], in_=w1_bf[g][:])

        v_s = sbuf([P, S], U8, "v_s")
        nc.vector.tensor_copy(out=v_s[:], in_=tab_s[:].indirect(idx[:]))
        round_w1(0)
        quantize_w1(0)
        v_c = [sbuf([P, BANK], U32, "v_c%d" % u) for u in range(HALVES)]
        for u in range(HALVES):
            part = slice(u * BANK // PER_COLUMN, (u + 1) * BANK // PER_COLUMN)
            nc.vector.tensor_copy(out=v_c[u][:], in_=tab_w[:].indirect(idx[:, part]))

        wg_second = sbuf([P, S], F32, "wg_second", tag="w4_raw")
        for q in range(QUADS):
            nc.sync.dma_start(out=wg_second[quad(q), :], in_=wgs_rows[:, 1, :])
        load_page(1)
        wg_rest = sbuf([P, 2, S], F32, "wg_rest", tag="w1_bf0")
        for q in range(QUADS):
            nc.sync.dma_start(out=wg_rest[quad(q), :, :], in_=wgs_rows[:, 2:, :])
        wg = (wg_first[:], wg_second[:], wg_rest[:, 0, :], wg_rest[:, 1, :])
        b2_t = sbuf([P, GROUPS, PACK], F32, "b2_t", tag="thr_t")
        nc.sync.dma_start(out=b2_t[:], in_=b2.rearrange("(g p t) -> p g t", p=P, t=PACK))
        load_w1(1)
        load_page(2)

        w2_raw = {}
        w2_c = [sbuf([P, N], U32, "w2_c%d" % g) for g in range(GROUPS)]
        w2_s = [sbuf([P, N], U8, "w2_s%d" % g) for g in range(GROUPS)]

        def load_w2(g):
            w2_raw[g] = sbuf([P, PACK, N], F32, "w2_raw%d" % g, tag="low%d1" % (g + 1))
            nc.sync.dma_start(out=w2_raw[g][:], in_=w2_rows[g])

        def quantize_w2(g, part):
            lo, hi = W2_PARTS[part]
            grouped = sbuf([P, PACK * (hi - lo)], BF16, "w2_bf%d_%d" % (g, part), tag="w2_bf%d" % part)
            nc.scalar.copy(
                out=grouped[:].rearrange("p (a i j) -> p a j i", i=LINE, j=PACK),
                in_=w2_raw[g][:, :, lo:hi].rearrange("p j (a i) -> p a j i", i=LINE),
            )
            nc.vector.quantize_mx(out=w2_c[g][:, lo:hi].bitcast(FP8X4), scales=w2_s[g][:, lo:hi], in_=grouped[:])

        h = {}

        def make_h(s):
            g, t = divmod(s, PACK)
            w1_cols = slice(t * P, (t + 1) * P)
            first = g * PASS + t * P
            shift = neg_thr[:, g, t : t + 1]
            h[s] = sbuf([P, S], F32, "h%d" % s, tag="h")
            for u in range(HALVES):
                half = slice(u * BANK, (u + 1) * BANK)
                left = psum.tile([P, BANK], F32, name="left%d_%d" % (s, u), tag="bank%d" % u)
                nc.tensor.matmul_mx(
                    out=left[:], lhsT=w1_c[g][:, w1_cols].bitcast(FP8X4), lhsT_scale=w1_s[g][:, w1_cols],
                    rhs=v_c[u][:].bitcast(FP8X4), rhs_scale=v_s[:, half], start=True, stop=True,
                )
                low = sbuf([P, BANK], F32, "low%d%d" % (s, u), tag=None if (s, u) in OWN_LOW else "low%d" % u)
                nc.scalar.activation(out=low[:], in_=left[:], func=ACT.Identity, bias=shift, scale=1.0)
                right = psum.tile([P, BANK], F32, name="right%d_%d" % (s, u), tag="bank%d" % (HALVES + u))
                nc.tensor.matmul_mx(
                    out=right[:], lhsT=w4_c[:, 2 * first : 2 * (first + P)].bitcast(FP4X4),
                    lhsT_scale=w4_s[:, first : first + P],
                    rhs=v_c[u][:].bitcast(FP8X4), rhs_scale=v_s[:, half], start=True, stop=True,
                )
                nc.vector.scalar_tensor_tensor(
                    out=h[s][:, half], in0=right[:], scalar=shift, in1=low[:], op0=ALU.add, op1=ALU.min
                )

        def scatter(s):
            g, t = divmod(s, PACK)
            nc.vector.tensor_tensor(out=pages[s][:].indirect(idx2[:]), in0=h[s][:], in1=wg[t], op=ALU.mult)
            nc.sync.dma_start(out=out_rows[g, t], in_=pages[s][:])

        x_bf = [sbuf([P, M, PACK], BF16, "x_bf%d" % g) for g in range(GROUPS)]
        x_c = [sbuf([P, M], U32, "x_c%d" % g) for g in range(GROUPS)]
        x_s = [sbuf([P, M], U8, "x_s%d" % g) for g in range(GROUPS)]

        def pick(s):
            g, t = divmod(s, PACK)
            bias = b2_t[:, g, t : t + 1]
            picked = sbuf([P, M], F32, "picked%d" % s, tag="low0" if s else None)
            nc.vector.tensor_copy(out=picked[:], in_=pages[s][:].indirect(idx3[:]))
            if s == SLICES - 1:
                nc.vector.tensor_scalar(out=x_bf[g][:, :, t], in0=picked[:], scalar1=bias, scalar2=None, op0=ALU.add)
            else:
                nc.scalar.activation(out=x_bf[g][:, :, t], in_=picked[:], func=ACT.Identity, bias=bias, scale=1.0)
            if t == PACK - 1:
                nc.vector.quantize_mx(
                    out=x_c[g][:].bitcast(FP8X4), scales=x_s[g][:], in_=x_bf[g][:].rearrange("p m t -> p (m t)")
                )

        pairs = {}
        woven = {}
        planes = {}

        def round_page(s):
            g, t = divmod(s, PACK)
            for c in range(CHUNKS):
                if t == 0:
                    pairs[g, c] = sbuf([P, 2, CHUNK, 2], BF16, "pairs%d_%d" % (g, c), tag="pairs%d" % c)
                nc.scalar.copy(out=pairs[g, c][:, t // 2, :, t % 2], in_=pages[s][:, c * CHUNK : (c + 1) * CHUNK])

        def weave(g, c, copy):
            woven[g, c] = sbuf([P, CHUNK * PACK], BF16, "woven%d_%d" % (g, c), tag="woven%d" % c)
            rows = pairs[g, c][:].rearrange("p u m e -> p (u m e)").bitcast(F32)
            copy(
                out=woven[g, c][:].bitcast(F32).rearrange("p (a i u) -> p a u i", i=LINE, u=2),
                in_=rows.rearrange("p (u a i) -> p a u i", i=LINE, u=2),
            )

        def quantize_page(g, c):
            if c == 0:
                planes[g] = (
                    sbuf([P, T2], U32, "page_c%d" % g, tag="w4_s_raw" if g == 0 else None),
                    sbuf([P, T2], U8, "page_s%d" % g),
                )
            codes, scales = planes[g]
            words = out_2[g].rearrange("p c i -> p (c i)").bitcast(I32)
            cols = slice(c * CHUNK, (c + 1) * CHUNK)
            nc.vector.quantize_mx(out=codes[:, cols].bitcast(FP8X4), scales=scales[:, cols], in_=woven[g, c][:])
            nc.sync.dma_start(out=words[:, cols], in_=codes[:, cols].bitcast(I32))
            if c == CHUNKS - 1:
                for q in range(QUADS):
                    nc.sync.dma_start(
                        out=out_3[g, scale_rows(q), :].bitcast(I32), in_=scales[quad(q, SCALE_ROWS), :].bitcast(I32)
                    )

        tones = {}
        spare_banks = BANKS - 2 * HALVES

        def tone_pass(g, n):
            if g == 0:
                tones[n] = psum.tile([P, M], F32, name="tone%d" % n, tag="bank%d" % ((2 * HALVES + n) % BANKS))
            cols = slice(n * P, (n + 1) * P)
            nc.tensor.matmul_mx(
                out=tones[n][:], lhsT=w2_c[g][:, cols].bitcast(FP8X4), lhsT_scale=w2_s[g][:, cols],
                rhs=x_c[g][:].bitcast(FP8X4), rhs_scale=x_s[g][:], start=(g == 0), stop=(g == GROUPS - 1),
            )

        def finish(n):
            size = sbuf([P, M], F32, "size%d" % n, tag="size", bufs=2)
            nc.scalar.activation(out=size[:], in_=tones[n][:], func=ACT.Abs)
            cosine = sbuf([P, M], F32, "cosine%d" % n, tag="cosine", bufs=3)
            nc.scalar.activation(out=cosine[:], in_=size[:], func=ACT.Sin, scale=-1.0, bias=math.pi / 2)
            y = sbuf([P, M], F32, "y%d" % n)
            nc.vector.tensor_tensor(out=y[:], in0=tones[n][:], in1=cosine[:], op=ALU.mult)
            nc.sync.dma_start(out=out_0[n * P : (n + 1) * P, :], in_=y[:])

        def step(s):
            scatter(s)
            if s + 1 < SLICES:
                make_h(s + 1)
            pick(s)

        make_h(0)
        load_page(3)
        load_page(4)
        step(0)
        load_page(5)
        load_w2(0)
        load_page(6)
        round_w1(1)
        round_page(0)
        step(1)
        load_w2(1)
        load_page(7)
        round_page(1)
        step(2)
        quantize_w1(1)
        round_page(2)
        quantize_w2(0, 0)
        step(3)
        round_page(3)
        quantize_w2(0, 1)
        step(4)
        for c in range(CHUNKS):
            weave(0, c, nc.scalar.copy)
        step(5)
        round_page(4)
        quantize_w2(1, 0)
        for n in range(spare_banks):
            tone_pass(0, n)
        step(6)
        for n in range(spare_banks, TILES):
            tone_pass(0, n)
        round_page(5)
        quantize_w2(1, 1)
        round_page(6)
        for c in range(CHUNKS):
            quantize_page(0, c)
        step(7)

        for n in range(TILES):
            tone_pass(1, n)
        round_page(SLICES - 1)
        for n in range(TILES):
            finish(n)
            if n < CHUNKS:
                weave(1, n, nc.vector.tensor_copy)
                quantize_page(1, n)
